import numpy as np
import ml_dtypes


def mxq(x, axis, fmt="e4m3"):
    dtype, down = {"e4m3": (ml_dtypes.float8_e4m3fn, 7), "e5m2": (ml_dtypes.float8_e5m2, 14)}[fmt]
    v = np.moveaxis(np.asarray(x, np.float32).astype(ml_dtypes.bfloat16).astype(np.float64), axis, -1)
    blocks = v.reshape(v.shape[:-1] + (-1, 32))
    amax = np.abs(blocks).max(-1, keepdims=True)
    byte = np.maximum(np.where(amax > 0, np.frexp(amax)[1] - 1 + 127, 0) - down, 1)
    scale = np.exp2(byte - 127.0)
    codes = (blocks / scale).astype(np.float32).astype(dtype).astype(np.float64)
    return np.moveaxis((codes * scale).reshape(v.shape), -1, axis)


WIDE = False


def mx_kscale(k):
    if not WIDE:
        return np.ones(k)
    levels = np.array([10, -10, 5, -5, 0])
    if k % 512:
        return np.exp2(np.random.permutation(np.resize(levels, k // 32))).repeat(32)
    a = np.empty((k // 512, 16))
    for p in range(k // 512):
        a[p, :8] = np.random.permutation(np.resize(levels, 8))
        for g in range(8):
            far = levels[np.abs(levels - a[p, g]) >= 10]
            a[p, g + 8] = far[np.random.randint(len(far))]
    return np.exp2(a.ravel()).repeat(32)


def f64(x):
    return np.asarray(x).astype(np.float64)


def striped(idx):
    return np.tile(np.asarray(idx).reshape(-1, 16).T, (8, 1)).astype(np.uint16)


def unstriped(offs):
    return offs[:16].T.reshape(-1).astype(np.int64)


E2M1 = np.array([0.0, 0.5, 1.0, 1.5, 2.0, 3.0, 4.0, 6.0, -0.0, -0.5, -1.0, -1.5, -2.0, -3.0, -4.0, -6.0])


def pack_weight(w, fmt):
    k, n = w.shape
    w = f64(np.asarray(w, np.float32).astype(ml_dtypes.bfloat16)).reshape(k // 32, 32, n)
    amax = np.abs(w).max(1)
    if fmt == "e4m3":
        byte = np.frexp(amax)[1] - 1 + 127 - 7
    else:
        mant, ex = np.frexp(amax / 6.0)
        byte = np.where(mant > 0.5, ex, ex - 1) + 127
    byte = np.clip(np.where(amax > 0, byte, 1), 1, 254)
    scaled = (w * np.exp2(127.0 - byte)[:, None, :]).reshape(k, n).astype(np.float32)
    by_word = np.ascontiguousarray(scaled.reshape(k // 512, 128, 4, n).transpose(0, 1, 3, 2))
    if fmt == "e4m3":
        words = by_word.astype(ml_dtypes.float8_e4m3fn).view(np.uint8)
    else:
        c = by_word.astype(ml_dtypes.float4_e2m1fn).view(np.uint8) & 0xF
        words = (c[..., 0::2] | (c[..., 1::2] << 4)).reshape(k // 512, 128, 2 * n)
    return np.ascontiguousarray(words), np.ascontiguousarray(byte.astype(np.uint8).reshape(k // 512, 16, n))


def unpack_weight(words, scales, fmt):
    g, _, n = scales.shape
    words = np.ascontiguousarray(words).reshape(g, 128, n, -1)
    if fmt == "e4m3":
        vals = words.view(ml_dtypes.float8_e4m3fn).astype(np.float64)
    else:
        nib = np.empty((g, 128, n, 4), np.uint8)
        nib[..., 0::2] = words & 0xF
        nib[..., 1::2] = words >> 4
        vals = E2M1[nib]
    vals = vals * np.repeat(np.exp2(scales.astype(np.float64) - 127.0), 8, axis=1)[..., None]
    return vals.transpose(0, 1, 3, 2).reshape(g * 512, n)


D, E, T, I, Q = 512, 512, 2048, 512, 128


def setup_inputs():
    n = np.random.standard_normal
    idx = np.random.permutation(T)[:I]
    fd = mx_kscale(D)
    fi = mx_kscale(I)
    ti = np.ones(T)
    ti[idx] = fi
    keysp = pack_weight(n((D, T)) / fd[:, None], "e2m1")
    return {
        "query": (n((D, Q)) * 1.0 / np.sqrt(D) * fd[:, None]).astype(np.float32),
        "keys_words": keysp[0],
        "keys_scales": keysp[1],
        "floor": (np.random.uniform(0.05, 0.3, (Q, 1))).astype(np.float32),
        "reserve": (np.random.uniform(20.0, 100.0, (Q, 1))).astype(np.float32),
        "os": (np.random.uniform(4.0, 16.0, (1, I)) * fi).astype(np.float32),
        "vals": (n((E, T)) / ti).astype(np.float32),
        "offs": striped(idx),
    }


def reference(query, keys_words, keys_scales, floor, reserve, os, vals, offs):
    idx = unstriped(offs)
    keysu = unpack_weight(keys_words, keys_scales, "e2m1")
    queryq = mxq(f64(query), 0, "e4m3")
    keysidxg = keysu[:, idx]
    a = queryq.T @ keysidxg
    p = np.square(a) + f64(floor)
    z = np.sum(p, axis=1, keepdims=True) + f64(reserve)
    w = p / z
    wo1 = w * f64(os)
    wt1 = wo1.T
    vt1 = f64(vals)[:, idx].T
    wt1q = mxq(wt1, 0, "e4m3")
    vt1q = mxq(vt1, 0, "e4m3")
    o = wt1q.T @ vt1q
    return o

@@ -1,0 +1,150 @@
+from contextlib import ExitStack
+
+import concourse.mybir as mybir
+from concourse.masks import make_identity
+
+D, E, T, I, Q = 512, 512, 2048, 512, 128
+FLOPS = 2 * Q * I * D + 2 * Q * E * I
+
+F32 = mybir.dt.float32
+BF16 = mybir.dt.bfloat16
+I32 = mybir.dt.int32
+U32 = mybir.dt.uint32
+U16 = mybir.dt.uint16
+U8 = mybir.dt.uint8
+FP8X4 = mybir.dt.float8_e4m3fn_x4
+FP4X4 = mybir.dt.float4_e2m1fn_x4
+ALU = mybir.AluOpType
+ACT = mybir.ActivationFunctionType
+
+P = 128
+PACK = 4
+E_TILES = E // P
+
+
+def tile_attend_squareshares_kernel(tc, query, keys_words, keys_scales, floor, reserve, slot_factor, vals, offs, out):
+    nc = tc.nc
+    with ExitStack() as ctx:
+        keep = ctx.enter_context(tc.tile_pool(name="keep", bufs=1))
+        pools = ctx.enter_context(tc.tile_pool(name="pools", bufs=3))
+        work = ctx.enter_context(tc.tile_pool(name="work", bufs=4))
+        psum_one = ctx.enter_context(tc.psum_pool(name="psum_one", bufs=1))
+        psum_ring = ctx.enter_context(tc.psum_pool(name="psum_ring", bufs=3))
+
+        offsets = keep.tile([P, I // 16], U16, name="offsets")
+        nc.sync.dma_start(offsets[:], offs)
+
+        key_scale_pool = keep.tile([P, T], U8, name="key_scale_pool", align_bytes=64)
+        nc.vector.memset(key_scale_pool[:].bitcast(I32), 0)
+        for quad in range(4):
+            nc.scalar.dma_start(
+                key_scale_pool[32 * quad : 32 * quad + 4, :].bitcast(I32),
+                keys_scales[0, 4 * quad : 4 * quad + 4, :].bitcast(I32),
+            )
+
+        key_word_pool = keep.tile([P, T], U16, name="key_word_pool", align_bytes=64)
+        nc.sync.dma_start(key_word_pool[:].bitcast(I32), keys_words[0].bitcast(I32))
+        q_raw = keep.tile([P, PACK, Q], F32, name="q_raw")
+        nc.sync.dma_start(q_raw[:], query.rearrange("(p t) q -> p t q", t=PACK))
+
+        floor_col = keep.tile([P, 1], F32, name="floor_col")
+        nc.gpsimd.dma_start(floor_col[:], floor)
+        reserve_col = keep.tile([P, 1], F32, name="reserve_col")
+        nc.gpsimd.dma_start(reserve_col[:], reserve)
+        os_cols = keep.tile([P, PACK], F32, name="os_cols")
+        nc.gpsimd.dma_start(os_cols[:], slot_factor.rearrange("o (p t) -> (o p) t", t=PACK))
+
+        identity = keep.tile([P, P], F32, name="identity")
+        make_identity(nc, identity[:])
+        warm = keep.tile([P, 1], F32, name="warm")
+        nc.scalar.activation(warm[:], identity[:, 0:1], ACT.Square)
+
+        def load_values(c):
+            value_pool = pools.tile([P, T], F32, name="value_pool")
+            nc.sync.dma_start(value_pool[:], vals[c * P : (c + 1) * P, :])
+            return value_pool
+
+        value_pools = [load_values(c) for c in range(E_TILES - 1)]
+
+        key_words = keep.tile([P, I], U16, name="key_words", align_bytes=64)
+        nc.vector.tensor_copy(key_words[:], key_word_pool[:].indirect(offsets[:]))
+        q_grouped = keep.tile([P, Q, PACK], BF16, name="q_grouped", align_bytes=64)
+        nc.scalar.copy(q_grouped[:], q_raw[:].rearrange("p t q -> p q t"))
+        key_scales = keep.tile([P, I], U8, name="key_scales", align_bytes=64)
+        nc.vector.tensor_copy(key_scales[:], key_scale_pool[:].indirect(offsets[:]))
+        q_codes = keep.tile([P, Q], U32, name="q_codes", align_bytes=64)
+        q_scales = keep.tile([P, Q], U8, name="q_scales", align_bytes=64)
+        nc.vector.quantize_mx(q_codes[:].bitcast(FP8X4), q_scales[:], q_grouped[:].rearrange("p q t -> p (q t)"))
+        scores = psum_one.tile([Q, I], F32, name="scores")
+        nc.tensor.matmul_mx(
+            scores[:], lhsT=q_codes[:].bitcast(FP8X4), lhsT_scale=q_scales[:],
+            rhs=key_words[:].bitcast(FP4X4), rhs_scale=key_scales[:], start=True, stop=True,
+        )
+
+        def gather_values(value_pool):
+            picked = work.tile([P, I], BF16, name="picked", align_bytes=64)
+            nc.vector.tensor_copy(picked[:], value_pool[:].indirect(offsets[:]))
+            pairs = picked[:].bitcast(F32)
+            turned = psum_ring.tile([P, 2, P], F32, name="turned")
+            for u in range(2):
+                nc.tensor.transpose(turned[:, u, :], pairs[:, u : I // 2 : 2], identity[:])
+            v_grouped = work.tile([P, P, 2], F32, name="v_grouped", align_bytes=64)
+            nc.scalar.copy(v_grouped[:], turned[:].rearrange("p u e -> p e u"))
+            return v_grouped
+
+        def quantize_values(v_grouped):
+            v_codes = work.tile([P, P], U32, name="v_codes", align_bytes=64)
+            v_scales = work.tile([P, P], U8, name="v_scales", align_bytes=64)
+            nc.vector.quantize_mx(
+                v_codes[:].bitcast(FP8X4), v_scales[:], v_grouped[:].rearrange("p e u -> p (e u)").bitcast(BF16)
+            )
+            return v_codes, v_scales
+
+        grouped = [gather_values(value_pools[0])]
+        value_pools.append(load_values(E_TILES - 1))
+
+        squares = keep.tile([Q, PACK, P], F32, name="squares")
+        square_sum = keep.tile([Q, 1], F32, name="square_sum")
+        nc.scalar.activation(
+            squares[:], scores[:].rearrange("q (p t) -> q t p", t=PACK), ACT.Square, accum_out=square_sum[:]
+        )
+        rest = keep.tile([Q, 1], F32, name="rest")
+        nc.vector.scalar_tensor_tensor(rest[:], floor_col[:], float(I), reserve_col[:], ALU.mult, ALU.add)
+        total = keep.tile([Q, 1], F32, name="total")
+        nc.vector.tensor_tensor(total[:], square_sum[:], rest[:], ALU.add)
+        inverse = keep.tile([Q, 1], F32, name="inverse")
+        nc.vector.reciprocal(inverse[:], total[:])
+        shares = keep.tile([Q, PACK, P], F32, name="shares")
+        nc.vector.tensor_scalar(shares[:], squares[:], floor_col[:], inverse[:], ALU.add, ALU.mult)
+        shares_turned = psum_one.tile([P, PACK, Q], F32, name="shares_turned")
+        for t in range(PACK):
+            nc.tensor.transpose(shares_turned[:, t, :], shares[:, t, :], identity[:])
+        w_grouped = keep.tile([P, Q, PACK], BF16, name="w_grouped", align_bytes=64)
+        nc.vector.tensor_tensor(
+            w_grouped[:],
+            shares_turned[:].rearrange("p t q -> p q t"),
+            os_cols[:].unsqueeze(1).to_broadcast([P, Q, PACK]),
+            ALU.mult,
+        )
+        w_codes = keep.tile([P, Q], U32, name="w_codes", align_bytes=64)
+        w_scales = keep.tile([P, Q], U8, name="w_scales", align_bytes=64)
+        nc.vector.quantize_mx(w_codes[:].bitcast(FP8X4), w_scales[:], w_grouped[:].rearrange("p q t -> p (q t)"))
+
+        early = keep.tile([Q, E - P], F32, name="early")
+        last = keep.tile([Q, P], F32, name="last")
+        for c in range(E_TILES):
+            v_codes, v_scales = quantize_values(grouped[c])
+            if c + 1 < E_TILES:
+                grouped.append(gather_values(value_pools[c + 1]))
+            sums = psum_ring.tile([Q, P], F32, name="sums")
+            nc.tensor.matmul_mx(
+                sums[:], lhsT=w_codes[:].bitcast(FP8X4), lhsT_scale=w_scales[:],
+                rhs=v_codes[:].bitcast(FP8X4), rhs_scale=v_scales[:], start=True, stop=True,
+            )
+            if c + 1 < E_TILES:
+                nc.scalar.copy(early[:, c * P : (c + 1) * P], sums[:])
+            else:
+                nc.scalar.copy(last[:], sums[:])
+            if c + 2 == E_TILES:
+                nc.sync.dma_start(out[:, : E - P], early[:])
+        nc.sync.dma_start(out[:, E - P :], last[:])

@@ -20,39 +20,31 @@ ACT = mybir.ActivationFunctionType
 P = 128
 PACK = 4
 E_TILES = E // P
+POOL_BYTES = 4 * T
 
 
 def tile_attend_squareshares_kernel(tc, query, keys_words, keys_scales, floor, reserve, slot_factor, vals, offs, out):
     nc = tc.nc
     with ExitStack() as ctx:
         keep = ctx.enter_context(tc.tile_pool(name="keep", bufs=1))
-        pools = ctx.enter_context(tc.tile_pool(name="pools", bufs=3))
+        reused = ctx.enter_context(tc.tile_pool(name="reused", bufs=1))
         work = ctx.enter_context(tc.tile_pool(name="work", bufs=4))
         psum_one = ctx.enter_context(tc.psum_pool(name="psum_one", bufs=1))
         psum_ring = ctx.enter_context(tc.psum_pool(name="psum_ring", bufs=3))
 
-        offsets = keep.tile([P, I // 16], U16, name="offsets")
-        nc.sync.dma_start(offsets[:], offs)
-
         key_scale_pool = keep.tile([P, T], U8, name="key_scale_pool", align_bytes=64)
         nc.vector.memset(key_scale_pool[:].bitcast(I32), 0)
+        q_raw = keep.tile([P, PACK, Q], F32, name="q_raw")
+        nc.sync.dma_start(q_raw[:], query.rearrange("(p t) q -> p t q", t=PACK))
         for quad in range(4):
-            nc.scalar.dma_start(
+            nc.sync.dma_start(
                 key_scale_pool[32 * quad : 32 * quad + 4, :].bitcast(I32),
                 keys_scales[0, 4 * quad : 4 * quad + 4, :].bitcast(I32),
             )
-
-        key_word_pool = keep.tile([P, T], U16, name="key_word_pool", align_bytes=64)
+        offsets = keep.tile([P, I // 16], U16, name="offsets")
+        nc.sync.dma_start(offsets[:], offs)
+        key_word_pool = keep.tile([P, T], U16, name="key_word_pool", tag="before0", align_bytes=64)
         nc.sync.dma_start(key_word_pool[:].bitcast(I32), keys_words[0].bitcast(I32))
-        q_raw = keep.tile([P, PACK, Q], F32, name="q_raw")
-        nc.sync.dma_start(q_raw[:], query.rearrange("(p t) q -> p t q", t=PACK))
-
-        floor_col = keep.tile([P, 1], F32, name="floor_col")
-        nc.gpsimd.dma_start(floor_col[:], floor)
-        reserve_col = keep.tile([P, 1], F32, name="reserve_col")
-        nc.gpsimd.dma_start(reserve_col[:], reserve)
-        os_cols = keep.tile([P, PACK], F32, name="os_cols")
-        nc.gpsimd.dma_start(os_cols[:], slot_factor.rearrange("o (p t) -> (o p) t", t=PACK))
 
         identity = keep.tile([P, P], F32, name="identity")
         make_identity(nc, identity[:])
@@ -60,14 +52,20 @@ def tile_attend_squareshares_kernel(tc, query, keys_words, keys_scales, floor, r
         nc.scalar.activation(warm[:], identity[:, 0:1], ACT.Square)
 
         def load_values(c):
-            value_pool = pools.tile([P, T], F32, name="value_pool")
+            value_pool = reused.tile([P, T], F32, name=f"value_pool{c}", offset=POOL_BYTES * c, align_bytes=64)
             nc.sync.dma_start(value_pool[:], vals[c * P : (c + 1) * P, :])
             return value_pool
 
-        value_pools = [load_values(c) for c in range(E_TILES - 1)]
+        value_pools = [load_values(0)]
+        floor_col = keep.tile([P, 1], F32, name="floor_col")
+        nc.sync.dma_start(floor_col[:], floor)
+        reserve_col = keep.tile([P, 1], F32, name="reserve_col")
+        nc.sync.dma_start(reserve_col[:], reserve)
+        os_cols = keep.tile([P, PACK], F32, name="os_cols")
+        nc.sync.dma_start(os_cols[:], slot_factor.rearrange("o (p t) -> (o p) t", t=PACK))
 
-        key_words = keep.tile([P, I], U16, name="key_words", align_bytes=64)
-        nc.vector.tensor_copy(key_words[:], key_word_pool[:].indirect(offsets[:]))
+        value_pools.extend(load_values(c) for c in range(1, E_TILES))
+
         q_grouped = keep.tile([P, Q, PACK], BF16, name="q_grouped", align_bytes=64)
         nc.scalar.copy(q_grouped[:], q_raw[:].rearrange("p t q -> p q t"))
         key_scales = keep.tile([P, I], U8, name="key_scales", align_bytes=64)
@@ -75,51 +73,62 @@ def tile_attend_squareshares_kernel(tc, query, keys_words, keys_scales, floor, r
         q_codes = keep.tile([P, Q], U32, name="q_codes", align_bytes=64)
         q_scales = keep.tile([P, Q], U8, name="q_scales", align_bytes=64)
         nc.vector.quantize_mx(q_codes[:].bitcast(FP8X4), q_scales[:], q_grouped[:].rearrange("p q t -> p (q t)"))
+        key_words = keep.tile([P, I], U16, name="key_words", align_bytes=64)
+        nc.vector.tensor_copy(key_words[:], key_word_pool[:].indirect(offsets[:]))
         scores = psum_one.tile([Q, I], F32, name="scores")
         nc.tensor.matmul_mx(
             scores[:], lhsT=q_codes[:].bitcast(FP8X4), lhsT_scale=q_scales[:],
             rhs=key_words[:].bitcast(FP4X4), rhs_scale=key_scales[:], start=True, stop=True,
         )
 
-        def gather_values(value_pool):
-            picked = work.tile([P, I], BF16, name="picked", align_bytes=64)
-            nc.vector.tensor_copy(picked[:], value_pool[:].indirect(offsets[:]))
+        def gather_values(c):
+            if c >= 2:
+                picked = reused.tile([P, I], BF16, name=f"picked{c}", offset=POOL_BYTES * (c - 1) + 1024, align_bytes=64)
+            else:
+                picked = keep.tile([P, I], BF16, name=f"picked{c}", tag=f"before{c}", align_bytes=64)
+            nc.vector.tensor_copy(picked[:], value_pools[c][:].indirect(offsets[:]))
             pairs = picked[:].bitcast(F32)
-            turned = psum_ring.tile([P, 2, P], F32, name="turned")
+            if c == 0:
+                turned = psum_one.tile([P, 2, P], F32, name="turned0", tag="scores")
+            else:
+                turned = psum_ring.tile([P, 2, P], F32, name="turned")
             for u in range(2):
                 nc.tensor.transpose(turned[:, u, :], pairs[:, u : I // 2 : 2], identity[:])
             v_grouped = work.tile([P, P, 2], F32, name="v_grouped", align_bytes=64)
             nc.scalar.copy(v_grouped[:], turned[:].rearrange("p u e -> p e u"))
             return v_grouped
 
-        def quantize_values(v_grouped):
-            v_codes = work.tile([P, P], U32, name="v_codes", align_bytes=64)
+        def quantize_values(c):
+            v_grouped = grouped[c]
+            if c + 1 < E_TILES:
+                v_codes = reused.tile([P, P], U32, name=f"v_codes{c}", offset=POOL_BYTES * (c + 1), align_bytes=64)
+            else:
+                v_codes = work.tile([P, P], U32, name="v_codes", align_bytes=64)
             v_scales = work.tile([P, P], U8, name="v_scales", align_bytes=64)
             nc.vector.quantize_mx(
                 v_codes[:].bitcast(FP8X4), v_scales[:], v_grouped[:].rearrange("p e u -> p (e u)").bitcast(BF16)
             )
             return v_codes, v_scales
 
-        grouped = [gather_values(value_pools[0])]
-        value_pools.append(load_values(E_TILES - 1))
-
-        squares = keep.tile([Q, PACK, P], F32, name="squares")
+        squares = keep.tile([Q, PACK, P], F32, name="squares", tag="before1", align_bytes=64)
         square_sum = keep.tile([Q, 1], F32, name="square_sum")
         nc.scalar.activation(
             squares[:], scores[:].rearrange("q (p t) -> q t p", t=PACK), ACT.Square, accum_out=square_sum[:]
         )
+        grouped = [gather_values(0)]
         rest = keep.tile([Q, 1], F32, name="rest")
-        nc.vector.scalar_tensor_tensor(rest[:], floor_col[:], float(I), reserve_col[:], ALU.mult, ALU.add)
-        total = keep.tile([Q, 1], F32, name="total")
+        nc.gpsimd.tensor_scalar(rest[:], floor_col[:], float(I), reserve_col[:], ALU.mult, ALU.add)
+        total = reused.tile([Q, 1], F32, name="total", offset=0, align_bytes=64)
         nc.vector.tensor_tensor(total[:], square_sum[:], rest[:], ALU.add)
         inverse = keep.tile([Q, 1], F32, name="inverse")
         nc.vector.reciprocal(inverse[:], total[:])
         shares = keep.tile([Q, PACK, P], F32, name="shares")
         nc.vector.tensor_scalar(shares[:], squares[:], floor_col[:], inverse[:], ALU.add, ALU.mult)
+        grouped.append(gather_values(1))
         shares_turned = psum_one.tile([P, PACK, Q], F32, name="shares_turned")
         for t in range(PACK):
             nc.tensor.transpose(shares_turned[:, t, :], shares[:, t, :], identity[:])
-        w_grouped = keep.tile([P, Q, PACK], BF16, name="w_grouped", align_bytes=64)
+        w_grouped = reused.tile([P, Q, PACK], BF16, name="w_grouped", offset=POOL_BYTES + 1024, align_bytes=64)
         nc.vector.tensor_tensor(
             w_grouped[:],
             shares_turned[:].rearrange("p t q -> p q t"),
@@ -130,21 +139,22 @@ def tile_attend_squareshares_kernel(tc, query, keys_words, keys_scales, floor, r
         w_scales = keep.tile([P, Q], U8, name="w_scales", align_bytes=64)
         nc.vector.quantize_mx(w_codes[:].bitcast(FP8X4), w_scales[:], w_grouped[:].rearrange("p q t -> p (q t)"))
 
-        early = keep.tile([Q, E - P], F32, name="early")
-        last = keep.tile([Q, P], F32, name="last")
-        for c in range(E_TILES):
-            v_codes, v_scales = quantize_values(grouped[c])
-            if c + 1 < E_TILES:
-                grouped.append(gather_values(value_pools[c + 1]))
+        def multiply(c, result):
+            v_codes, v_scales = quantize_values(c)
             sums = psum_ring.tile([Q, P], F32, name="sums")
             nc.tensor.matmul_mx(
                 sums[:], lhsT=w_codes[:].bitcast(FP8X4), lhsT_scale=w_scales[:],
                 rhs=v_codes[:].bitcast(FP8X4), rhs_scale=v_scales[:], start=True, stop=True,
             )
-            if c + 1 < E_TILES:
-                nc.scalar.copy(early[:, c * P : (c + 1) * P], sums[:])
-            else:
-                nc.scalar.copy(last[:], sums[:])
-            if c + 2 == E_TILES:
-                nc.sync.dma_start(out[:, : E - P], early[:])
-        nc.sync.dma_start(out[:, E - P :], last[:])
+            nc.scalar.copy(result, sums[:])
+
+        early = keep.tile([Q, 2 * P], F32, name="early")
+        grouped.append(gather_values(2))
+        for c in range(2):
+            multiply(c, early[:, c * P : (c + 1) * P])
+        nc.sync.dma_start(out[:, : 2 * P], early[:])
+        grouped.append(gather_values(3))
+        for c in range(2, E_TILES):
+            late = work.tile([Q, P], F32, name="late")
+            multiply(c, late[:])
+            nc.sync.dma_start(out[:, c * P : (c + 1) * P], late[:])

@@ -28,7 +28,7 @@ def tile_attend_squareshares_kernel(tc, query, keys_words, keys_scales, floor, r
     with ExitStack() as ctx:
         keep = ctx.enter_context(tc.tile_pool(name="keep", bufs=1))
         reused = ctx.enter_context(tc.tile_pool(name="reused", bufs=1))
-        work = ctx.enter_context(tc.tile_pool(name="work", bufs=4))
+        work = ctx.enter_context(tc.tile_pool(name="work", bufs=5))
         psum_one = ctx.enter_context(tc.psum_pool(name="psum_one", bufs=1))
         psum_ring = ctx.enter_context(tc.psum_pool(name="psum_ring", bufs=3))
 
@@ -36,11 +36,8 @@ def tile_attend_squareshares_kernel(tc, query, keys_words, keys_scales, floor, r
         nc.vector.memset(key_scale_pool[:].bitcast(I32), 0)
         q_raw = keep.tile([P, PACK, Q], F32, name="q_raw")
         nc.sync.dma_start(q_raw[:], query.rearrange("(p t) q -> p t q", t=PACK))
-        for quad in range(4):
-            nc.sync.dma_start(
-                key_scale_pool[32 * quad : 32 * quad + 4, :].bitcast(I32),
-                keys_scales[0, 4 * quad : 4 * quad + 4, :].bitcast(I32),
-            )
+        for r in range(4):
+            nc.sync.dma_start(key_scale_pool[r:P:32, :].bitcast(I32), keys_scales[0, r:16:4, :].bitcast(I32))
         offsets = keep.tile([P, I // 16], U16, name="offsets")
         nc.sync.dma_start(offsets[:], offs)
         key_word_pool = keep.tile([P, T], U16, name="key_word_pool", tag="before0", align_bytes=64)
@@ -57,12 +54,12 @@ def tile_attend_squareshares_kernel(tc, query, keys_words, keys_scales, floor, r
             return value_pool
 
         value_pools = [load_values(0)]
+        os_cols = keep.tile([P, PACK], F32, name="os_cols")
+        nc.gpsimd.dma_start(os_cols[:], slot_factor.rearrange("o (p t) -> (o p) t", t=PACK))
         floor_col = keep.tile([P, 1], F32, name="floor_col")
         nc.sync.dma_start(floor_col[:], floor)
         reserve_col = keep.tile([P, 1], F32, name="reserve_col")
         nc.sync.dma_start(reserve_col[:], reserve)
-        os_cols = keep.tile([P, PACK], F32, name="os_cols")
-        nc.sync.dma_start(os_cols[:], slot_factor.rearrange("o (p t) -> (o p) t", t=PACK))
 
         value_pools.extend(load_values(c) for c in range(1, E_TILES))
 
@@ -81,80 +78,84 @@ def tile_attend_squareshares_kernel(tc, query, keys_words, keys_scales, floor, r
             rhs=key_words[:].bitcast(FP4X4), rhs_scale=key_scales[:], start=True, stop=True,
         )
 
-        def gather_values(c):
-            if c >= 2:
-                picked = reused.tile([P, I], BF16, name=f"picked{c}", offset=POOL_BYTES * (c - 1) + 1024, align_bytes=64)
-            else:
-                picked = keep.tile([P, I], BF16, name=f"picked{c}", tag=f"before{c}", align_bytes=64)
-            nc.vector.tensor_copy(picked[:], value_pools[c][:].indirect(offsets[:]))
-            pairs = picked[:].bitcast(F32)
-            if c == 0:
-                turned = psum_one.tile([P, 2, P], F32, name="turned0", tag="scores")
-            else:
-                turned = psum_ring.tile([P, 2, P], F32, name="turned")
+        factors = psum_one.tile([P, PACK, P], F32, name="factors")
+        for t in range(PACK):
+            nc.tensor.transpose(factors[:, t, :], os_cols[:, t : t + 1].to_broadcast([P, P]), identity[:])
+
+        def in_slot_order(rows):
+            return rows[:].rearrange("x (u g m) -> x g u m", u=2, m=16)
+
+        def turn(rows, turned):
+            pairs = rows[:].bitcast(F32)
             for u in range(2):
-                nc.tensor.transpose(turned[:, u, :], pairs[:, u : I // 2 : 2], identity[:])
-            v_grouped = work.tile([P, P, 2], F32, name="v_grouped", align_bytes=64)
-            nc.scalar.copy(v_grouped[:], turned[:].rearrange("p u e -> p e u"))
-            return v_grouped
+                nc.tensor.transpose(turned[:, u, :], pairs[:, u * P : (u + 1) * P], identity[:])
+            grouped = work.tile([P, P, 2], F32, name="grouped", align_bytes=64)
+            nc.scalar.copy(grouped[:], turned[:].rearrange("p u e -> p e u"))
+            return grouped
 
-        def quantize_values(c):
-            v_grouped = grouped[c]
-            if c + 1 < E_TILES:
-                v_codes = reused.tile([P, P], U32, name=f"v_codes{c}", offset=POOL_BYTES * (c + 1), align_bytes=64)
-            else:
-                v_codes = work.tile([P, P], U32, name="v_codes", align_bytes=64)
-            v_scales = work.tile([P, P], U8, name="v_scales", align_bytes=64)
+        def gather_values(c, picked, turned):
+            nc.vector.tensor_copy(in_slot_order(picked), value_pools[c][:].indirect(offsets[:]))
+            return turn(picked, turned)
+
+        def quantize(grouped, codes):
+            scales = work.tile([P, P], U8, name="scales", align_bytes=64)
             nc.vector.quantize_mx(
-                v_codes[:].bitcast(FP8X4), v_scales[:], v_grouped[:].rearrange("p e u -> p (e u)").bitcast(BF16)
+                codes[:].bitcast(FP8X4), scales[:], grouped[:].rearrange("p e u -> p (e u)").bitcast(BF16)
             )
-            return v_codes, v_scales
+            return codes, scales
 
-        squares = keep.tile([Q, PACK, P], F32, name="squares", tag="before1", align_bytes=64)
+        def after_gather(c, slot, shape, dtype, name):
+            return reused.tile(shape, dtype, name=name, offset=POOL_BYTES * c + 2048 * slot, align_bytes=64)
+
+        def ring_bank():
+            return psum_ring.tile([P, 2, P], F32, name="turned")
+
+        squares = keep.tile([Q, I], F32, name="squares")
         square_sum = keep.tile([Q, 1], F32, name="square_sum")
-        nc.scalar.activation(
-            squares[:], scores[:].rearrange("q (p t) -> q t p", t=PACK), ACT.Square, accum_out=square_sum[:]
-        )
-        grouped = [gather_values(0)]
+        nc.scalar.activation(squares[:], scores[:], ACT.Square, accum_out=square_sum[:])
+        picked0 = keep.tile([P, I], BF16, name="picked0", tag="before0", align_bytes=64)
+        nc.vector.tensor_copy(in_slot_order(picked0), value_pools[0][:].indirect(offsets[:]))
         rest = keep.tile([Q, 1], F32, name="rest")
         nc.gpsimd.tensor_scalar(rest[:], floor_col[:], float(I), reserve_col[:], ALU.mult, ALU.add)
-        total = reused.tile([Q, 1], F32, name="total", offset=0, align_bytes=64)
+        total = after_gather(0, 0, [Q, 1], F32, "total")
         nc.vector.tensor_tensor(total[:], square_sum[:], rest[:], ALU.add)
-        inverse = keep.tile([Q, 1], F32, name="inverse")
-        nc.vector.reciprocal(inverse[:], total[:])
-        shares = keep.tile([Q, PACK, P], F32, name="shares")
-        nc.vector.tensor_scalar(shares[:], squares[:], floor_col[:], inverse[:], ALU.add, ALU.mult)
-        grouped.append(gather_values(1))
-        shares_turned = psum_one.tile([P, PACK, Q], F32, name="shares_turned")
-        for t in range(PACK):
-            nc.tensor.transpose(shares_turned[:, t, :], shares[:, t, :], identity[:])
-        w_grouped = reused.tile([P, Q, PACK], BF16, name="w_grouped", offset=POOL_BYTES + 1024, align_bytes=64)
-        nc.vector.tensor_tensor(
-            w_grouped[:],
-            shares_turned[:].rearrange("p t q -> p q t"),
-            os_cols[:].unsqueeze(1).to_broadcast([P, Q, PACK]),
+        parts = keep.tile([Q, I], F32, name="parts", tag="before1", align_bytes=64)
+        nc.vector.scalar_tensor_tensor(
+            parts[:].rearrange("q (p t) -> q p t", t=PACK),
+            squares[:].rearrange("q (p t) -> q p t", t=PACK),
+            floor_col[:],
+            factors[:].rearrange("q t p -> q p t"),
+            ALU.add,
             ALU.mult,
         )
-        w_codes = keep.tile([P, Q], U32, name="w_codes", align_bytes=64)
-        w_scales = keep.tile([P, Q], U8, name="w_scales", align_bytes=64)
-        nc.vector.quantize_mx(w_codes[:].bitcast(FP8X4), w_scales[:], w_grouped[:].rearrange("p q t -> p (q t)"))
+        grouped0 = turn(picked0, psum_one.tile([P, 2, P], F32, name="turned0", tag="factors"))
+        inverse = keep.tile([Q, 1], F32, name="inverse")
+        nc.vector.reciprocal(inverse[:], total[:])
+        weights = keep.tile([Q, I], BF16, name="weights", align_bytes=64)
+        nc.vector.tensor_scalar(in_slot_order(weights), parts[:].rearrange("q (g u m) -> q g u m", u=2, m=16), inverse[:], None, ALU.mult)
+        w_grouped = turn(weights, ring_bank())
 
-        def multiply(c, result):
-            v_codes, v_scales = quantize_values(c)
+        picked1 = keep.tile([P, I], BF16, name="picked1", tag="before1", align_bytes=64)
+        grouped1 = gather_values(1, picked1, ring_bank())
+        v0 = quantize(grouped0, after_gather(1, 0, [P, P], U32, "codes0"))
+        grouped2 = gather_values(2, after_gather(1, 1, [P, I], BF16, "picked2"), ring_bank())
+        w_codes, w_scales = quantize(w_grouped, after_gather(2, 0, [P, Q], U32, "w_codes"))
+        v1 = quantize(grouped1, after_gather(2, 1, [P, P], U32, "codes1"))
+
+        def multiply(v, result):
             sums = psum_ring.tile([Q, P], F32, name="sums")
             nc.tensor.matmul_mx(
                 sums[:], lhsT=w_codes[:].bitcast(FP8X4), lhsT_scale=w_scales[:],
-                rhs=v_codes[:].bitcast(FP8X4), rhs_scale=v_scales[:], start=True, stop=True,
+                rhs=v[0][:].bitcast(FP8X4), rhs_scale=v[1][:], start=True, stop=True,
             )
             nc.scalar.copy(result, sums[:])
 
         early = keep.tile([Q, 2 * P], F32, name="early")
-        grouped.append(gather_values(2))
-        for c in range(2):
-            multiply(c, early[:, c * P : (c + 1) * P])
+        multiply(v0, early[:, :P])
+        multiply(v1, early[:, P:])
         nc.sync.dma_start(out[:, : 2 * P], early[:])
-        grouped.append(gather_values(3))
-        for c in range(2, E_TILES):
+        grouped3 = gather_values(3, after_gather(2, 2, [P, I], BF16, "picked3"), ring_bank())
+        for c, grouped in ((2, grouped2), (3, grouped3)):
             late = work.tile([Q, P], F32, name="late")
-            multiply(c, late[:])
+            multiply(quantize(grouped, after_gather(3, c - 2, [P, P], U32, f"codes{c}")), late[:])
             nc.sync.dma_start(out[:, c * P : (c + 1) * P], late[:])

@@ -32,37 +32,36 @@ def tile_attend_squareshares_kernel(tc, query, keys_words, keys_scales, floor, r
         psum_one = ctx.enter_context(tc.psum_pool(name="psum_one", bufs=1))
         psum_ring = ctx.enter_context(tc.psum_pool(name="psum_ring", bufs=3))
 
-        key_scale_pool = keep.tile([P, T], U8, name="key_scale_pool", align_bytes=64)
+        key_scale_pool = keep.tile([P, T], U8, name="key_scale_pool", tag="before0", align_bytes=64)
         nc.vector.memset(key_scale_pool[:].bitcast(I32), 0)
+        key_word_pool = keep.tile([P, T], U16, name="key_word_pool", align_bytes=64)
+        nc.sync.dma_start(key_word_pool[:].bitcast(I32), keys_words[0].bitcast(I32))
+        offsets = keep.tile([P, I // 16], U16, name="offsets")
+        nc.sync.dma_start(offsets[:], offs)
         q_raw = keep.tile([P, PACK, Q], F32, name="q_raw")
         nc.sync.dma_start(q_raw[:], query.rearrange("(p t) q -> p t q", t=PACK))
         for r in range(4):
             nc.sync.dma_start(key_scale_pool[r:P:32, :].bitcast(I32), keys_scales[0, r:16:4, :].bitcast(I32))
-        offsets = keep.tile([P, I // 16], U16, name="offsets")
-        nc.sync.dma_start(offsets[:], offs)
-        key_word_pool = keep.tile([P, T], U16, name="key_word_pool", tag="before0", align_bytes=64)
-        nc.sync.dma_start(key_word_pool[:].bitcast(I32), keys_words[0].bitcast(I32))
+
+        os_cols = keep.tile([P, PACK], F32, name="os_cols")
+        nc.gpsimd.dma_start(os_cols[:], slot_factor.rearrange("o (p t) -> (o p) t", t=PACK))
+        floor_col = keep.tile([P, 1], F32, name="floor_col")
+        nc.gpsimd.dma_start(floor_col[:], floor)
+        reserve_col = keep.tile([P, 1], F32, name="reserve_col")
+        nc.gpsimd.dma_start(reserve_col[:], reserve)
 
         identity = keep.tile([P, P], F32, name="identity")
         make_identity(nc, identity[:])
-        warm = keep.tile([P, 1], F32, name="warm")
-        nc.scalar.activation(warm[:], identity[:, 0:1], ACT.Square)
 
         def load_values(c):
             value_pool = reused.tile([P, T], F32, name=f"value_pool{c}", offset=POOL_BYTES * c, align_bytes=64)
             nc.sync.dma_start(value_pool[:], vals[c * P : (c + 1) * P, :])
             return value_pool
 
-        value_pools = [load_values(0)]
-        os_cols = keep.tile([P, PACK], F32, name="os_cols")
-        nc.gpsimd.dma_start(os_cols[:], slot_factor.rearrange("o (p t) -> (o p) t", t=PACK))
-        floor_col = keep.tile([P, 1], F32, name="floor_col")
-        nc.sync.dma_start(floor_col[:], floor)
-        reserve_col = keep.tile([P, 1], F32, name="reserve_col")
-        nc.sync.dma_start(reserve_col[:], reserve)
+        value_pools = [load_values(c) for c in range(E_TILES)]
 
-        value_pools.extend(load_values(c) for c in range(1, E_TILES))
-
+        key_words = keep.tile([P, I], U16, name="key_words", align_bytes=64)
+        nc.vector.tensor_copy(key_words[:], key_word_pool[:].indirect(offsets[:]))
         q_grouped = keep.tile([P, Q, PACK], BF16, name="q_grouped", align_bytes=64)
         nc.scalar.copy(q_grouped[:], q_raw[:].rearrange("p t q -> p q t"))
         key_scales = keep.tile([P, I], U8, name="key_scales", align_bytes=64)
@@ -70,8 +69,6 @@ def tile_attend_squareshares_kernel(tc, query, keys_words, keys_scales, floor, r
         q_codes = keep.tile([P, Q], U32, name="q_codes", align_bytes=64)
         q_scales = keep.tile([P, Q], U8, name="q_scales", align_bytes=64)
         nc.vector.quantize_mx(q_codes[:].bitcast(FP8X4), q_scales[:], q_grouped[:].rearrange("p q t -> p (q t)"))
-        key_words = keep.tile([P, I], U16, name="key_words", align_bytes=64)
-        nc.vector.tensor_copy(key_words[:], key_word_pool[:].indirect(offsets[:]))
         scores = psum_one.tile([Q, I], F32, name="scores")
         nc.tensor.matmul_mx(
             scores[:], lhsT=q_codes[:].bitcast(FP8X4), lhsT_scale=q_scales[:],
@@ -119,7 +116,7 @@ def tile_attend_squareshares_kernel(tc, query, keys_words, keys_scales, floor, r
         nc.gpsimd.tensor_scalar(rest[:], floor_col[:], float(I), reserve_col[:], ALU.mult, ALU.add)
         total = after_gather(0, 0, [Q, 1], F32, "total")
         nc.vector.tensor_tensor(total[:], square_sum[:], rest[:], ALU.add)
-        parts = keep.tile([Q, I], F32, name="parts", tag="before1", align_bytes=64)
+        parts = keep.tile([Q, I], F32, name="parts")
         nc.vector.scalar_tensor_tensor(
             parts[:].rearrange("q (p t) -> q p t", t=PACK),
             squares[:].rearrange("q (p t) -> q p t", t=PACK),
@@ -132,15 +129,15 @@ def tile_attend_squareshares_kernel(tc, query, keys_words, keys_scales, floor, r
         inverse = keep.tile([Q, 1], F32, name="inverse")
         nc.vector.reciprocal(inverse[:], total[:])
         weights = keep.tile([Q, I], BF16, name="weights", align_bytes=64)
-        nc.vector.tensor_scalar(in_slot_order(weights), parts[:].rearrange("q (g u m) -> q g u m", u=2, m=16), inverse[:], None, ALU.mult)
+        nc.scalar.activation(
+            in_slot_order(weights), parts[:].rearrange("q (g u m) -> q g u m", u=2, m=16), ACT.Copy, scale=inverse[:]
+        )
         w_grouped = turn(weights, ring_bank())
 
-        picked1 = keep.tile([P, I], BF16, name="picked1", tag="before1", align_bytes=64)
+        picked1 = after_gather(0, 0, [P, I], BF16, "picked1")
         grouped1 = gather_values(1, picked1, ring_bank())
-        v0 = quantize(grouped0, after_gather(1, 0, [P, P], U32, "codes0"))
-        grouped2 = gather_values(2, after_gather(1, 1, [P, I], BF16, "picked2"), ring_bank())
+        grouped2 = gather_values(2, after_gather(1, 0, [P, I], BF16, "picked2"), ring_bank())
         w_codes, w_scales = quantize(w_grouped, after_gather(2, 0, [P, Q], U32, "w_codes"))
-        v1 = quantize(grouped1, after_gather(2, 1, [P, P], U32, "codes1"))
 
         def multiply(v, result):
             sums = psum_ring.tile([Q, P], F32, name="sums")
@@ -150,12 +147,14 @@ def tile_attend_squareshares_kernel(tc, query, keys_words, keys_scales, floor, r
             )
             nc.scalar.copy(result, sums[:])
 
-        early = keep.tile([Q, 2 * P], F32, name="early")
-        multiply(v0, early[:, :P])
-        multiply(v1, early[:, P:])
-        nc.sync.dma_start(out[:, : 2 * P], early[:])
+        first = keep.tile([Q, P], F32, name="first")
+        multiply(quantize(grouped0, after_gather(2, 1, [P, P], U32, "codes0")), first[:])
+        nc.sync.dma_start(out[:, :P], first[:])
         grouped3 = gather_values(3, after_gather(2, 2, [P, I], BF16, "picked3"), ring_bank())
-        for c, grouped in ((2, grouped2), (3, grouped3)):
-            late = work.tile([Q, P], F32, name="late")
-            multiply(quantize(grouped, after_gather(3, c - 2, [P, P], U32, f"codes{c}")), late[:])
-            nc.sync.dma_start(out[:, c * P : (c + 1) * P], late[:])
+        middle = keep.tile([Q, 2 * P], F32, name="middle")
+        multiply(quantize(grouped1, after_gather(3, 0, [P, P], U32, "codes1")), middle[:, :P])
+        multiply(quantize(grouped2, after_gather(3, 1, [P, P], U32, "codes2")), middle[:, P:])
+        nc.sync.dma_start(out[:, P : 3 * P], middle[:])
+        last = keep.tile([Q, P], F32, name="last")
+        multiply(quantize(grouped3, after_gather(3, 2, [P, P], U32, "codes3")), last[:])
+        nc.sync.dma_start(out[:, 3 * P :], last[:])

from contextlib import ExitStack

import concourse.mybir as mybir
from concourse.masks import make_identity

D, E, T, I, Q = 512, 512, 2048, 512, 128
FLOPS = 2 * Q * I * D + 2 * Q * E * I

F32 = mybir.dt.float32
BF16 = mybir.dt.bfloat16
I32 = mybir.dt.int32
U32 = mybir.dt.uint32
U16 = mybir.dt.uint16
U8 = mybir.dt.uint8
FP8X4 = mybir.dt.float8_e4m3fn_x4
FP4X4 = mybir.dt.float4_e2m1fn_x4
ALU = mybir.AluOpType
ACT = mybir.ActivationFunctionType

P = 128
PACK = 4
E_TILES = E // P
POOL_BYTES = 4 * T


def tile_attend_squareshares_kernel(tc, query, keys_words, keys_scales, floor, reserve, slot_factor, vals, offs, out):
    nc = tc.nc
    with ExitStack() as ctx:
        keep = ctx.enter_context(tc.tile_pool(name="keep", bufs=1))
        reused = ctx.enter_context(tc.tile_pool(name="reused", bufs=1))
        work = ctx.enter_context(tc.tile_pool(name="work", bufs=5))
        psum_one = ctx.enter_context(tc.psum_pool(name="psum_one", bufs=1))
        psum_ring = ctx.enter_context(tc.psum_pool(name="psum_ring", bufs=3))

        key_scale_pool = keep.tile([P, T], U8, name="key_scale_pool", tag="before0", align_bytes=64)
        nc.vector.memset(key_scale_pool[:].bitcast(I32), 0)
        key_word_pool = keep.tile([P, T], U16, name="key_word_pool", align_bytes=64)
        nc.sync.dma_start(key_word_pool[:].bitcast(I32), keys_words[0].bitcast(I32))
        offsets = keep.tile([P, I // 16], U16, name="offsets")
        nc.sync.dma_start(offsets[:], offs)
        q_raw = keep.tile([P, PACK, Q], F32, name="q_raw")
        nc.sync.dma_start(q_raw[:], query.rearrange("(p t) q -> p t q", t=PACK))
        for r in range(4):
            nc.sync.dma_start(key_scale_pool[r:P:32, :].bitcast(I32), keys_scales[0, r:16:4, :].bitcast(I32))

        os_cols = keep.tile([P, PACK], F32, name="os_cols")
        nc.gpsimd.dma_start(os_cols[:], slot_factor.rearrange("o (p t) -> (o p) t", t=PACK))
        floor_col = keep.tile([P, 1], F32, name="floor_col")
        nc.gpsimd.dma_start(floor_col[:], floor)
        reserve_col = keep.tile([P, 1], F32, name="reserve_col")
        nc.gpsimd.dma_start(reserve_col[:], reserve)

        identity = keep.tile([P, P], F32, name="identity")
        make_identity(nc, identity[:])

        def load_values(c):
            value_pool = reused.tile([P, T], F32, name=f"value_pool{c}", offset=POOL_BYTES * c, align_bytes=64)
            nc.sync.dma_start(value_pool[:], vals[c * P : (c + 1) * P, :])
            return value_pool

        value_pools = [load_values(c) for c in range(E_TILES)]

        key_words = keep.tile([P, I], U16, name="key_words", align_bytes=64)
        nc.vector.tensor_copy(key_words[:], key_word_pool[:].indirect(offsets[:]))
        q_grouped = keep.tile([P, Q, PACK], BF16, name="q_grouped", align_bytes=64)
        nc.scalar.copy(q_grouped[:], q_raw[:].rearrange("p t q -> p q t"))
        key_scales = keep.tile([P, I], U8, name="key_scales", align_bytes=64)
        nc.vector.tensor_copy(key_scales[:], key_scale_pool[:].indirect(offsets[:]))
        q_codes = keep.tile([P, Q], U32, name="q_codes", align_bytes=64)
        q_scales = keep.tile([P, Q], U8, name="q_scales", align_bytes=64)
        nc.vector.quantize_mx(q_codes[:].bitcast(FP8X4), q_scales[:], q_grouped[:].rearrange("p q t -> p (q t)"))
        scores = psum_one.tile([Q, I], F32, name="scores")
        nc.tensor.matmul_mx(
            scores[:], lhsT=q_codes[:].bitcast(FP8X4), lhsT_scale=q_scales[:],
            rhs=key_words[:].bitcast(FP4X4), rhs_scale=key_scales[:], start=True, stop=True,
        )

        factors = psum_one.tile([P, PACK, P], F32, name="factors")
        for t in range(PACK):
            nc.tensor.transpose(factors[:, t, :], os_cols[:, t : t + 1].to_broadcast([P, P]), identity[:])

        def in_slot_order(rows):
            return rows[:].rearrange("x (u g m) -> x g u m", u=2, m=16)

        def turn(rows, turned):
            pairs = rows[:].bitcast(F32)
            for u in range(2):
                nc.tensor.transpose(turned[:, u, :], pairs[:, u * P : (u + 1) * P], identity[:])
            grouped = work.tile([P, P, 2], F32, name="grouped", align_bytes=64)
            nc.scalar.copy(grouped[:], turned[:].rearrange("p u e -> p e u"))
            return grouped

        def gather_values(c, picked, turned):
            nc.vector.tensor_copy(in_slot_order(picked), value_pools[c][:].indirect(offsets[:]))
            return turn(picked, turned)

        def quantize(grouped, codes):
            scales = work.tile([P, P], U8, name="scales", align_bytes=64)
            nc.vector.quantize_mx(
                codes[:].bitcast(FP8X4), scales[:], grouped[:].rearrange("p e u -> p (e u)").bitcast(BF16)
            )
            return codes, scales

        def after_gather(c, slot, shape, dtype, name):
            return reused.tile(shape, dtype, name=name, offset=POOL_BYTES * c + 2048 * slot, align_bytes=64)

        def ring_bank():
            return psum_ring.tile([P, 2, P], F32, name="turned")

        squares = keep.tile([Q, I], F32, name="squares")
        square_sum = keep.tile([Q, 1], F32, name="square_sum")
        nc.scalar.activation(squares[:], scores[:], ACT.Square, accum_out=square_sum[:])
        picked0 = keep.tile([P, I], BF16, name="picked0", tag="before0", align_bytes=64)
        nc.vector.tensor_copy(in_slot_order(picked0), value_pools[0][:].indirect(offsets[:]))
        rest = keep.tile([Q, 1], F32, name="rest")
        nc.gpsimd.tensor_scalar(rest[:], floor_col[:], float(I), reserve_col[:], ALU.mult, ALU.add)
        total = after_gather(0, 0, [Q, 1], F32, "total")
        nc.vector.tensor_tensor(total[:], square_sum[:], rest[:], ALU.add)
        parts = keep.tile([Q, I], F32, name="parts")
        nc.vector.scalar_tensor_tensor(
            parts[:].rearrange("q (p t) -> q p t", t=PACK),
            squares[:].rearrange("q (p t) -> q p t", t=PACK),
            floor_col[:],
            factors[:].rearrange("q t p -> q p t"),
            ALU.add,
            ALU.mult,
        )
        grouped0 = turn(picked0, psum_one.tile([P, 2, P], F32, name="turned0", tag="factors"))
        inverse = keep.tile([Q, 1], F32, name="inverse")
        nc.vector.reciprocal(inverse[:], total[:])
        weights = keep.tile([Q, I], BF16, name="weights", align_bytes=64)
        nc.scalar.activation(
            in_slot_order(weights), parts[:].rearrange("q (g u m) -> q g u m", u=2, m=16), ACT.Copy, scale=inverse[:]
        )
        w_grouped = turn(weights, ring_bank())

        picked1 = after_gather(0, 0, [P, I], BF16, "picked1")
        grouped1 = gather_values(1, picked1, ring_bank())
        grouped2 = gather_values(2, after_gather(1, 0, [P, I], BF16, "picked2"), ring_bank())
        w_codes, w_scales = quantize(w_grouped, after_gather(2, 0, [P, Q], U32, "w_codes"))

        def multiply(v, result):
            sums = psum_ring.tile([Q, P], F32, name="sums")
            nc.tensor.matmul_mx(
                sums[:], lhsT=w_codes[:].bitcast(FP8X4), lhsT_scale=w_scales[:],
                rhs=v[0][:].bitcast(FP8X4), rhs_scale=v[1][:], start=True, stop=True,
            )
            nc.scalar.copy(result, sums[:])

        first = keep.tile([Q, P], F32, name="first")
        multiply(quantize(grouped0, after_gather(2, 1, [P, P], U32, "codes0")), first[:])
        nc.sync.dma_start(out[:, :P], first[:])
        grouped3 = gather_values(3, after_gather(2, 2, [P, I], BF16, "picked3"), ring_bank())
        middle = keep.tile([Q, 2 * P], F32, name="middle")
        multiply(quantize(grouped1, after_gather(3, 0, [P, P], U32, "codes1")), middle[:, :P])
        multiply(quantize(grouped2, after_gather(3, 1, [P, P], U32, "codes2")), middle[:, P:])
        nc.sync.dma_start(out[:, P : 3 * P], middle[:])
        last = keep.tile([Q, P], F32, name="last")
        multiply(quantize(grouped3, after_gather(3, 2, [P, P], U32, "codes3")), last[:])
        nc.sync.dma_start(out[:, 3 * P :], last[:])
